import numpy as np
import ml_dtypes


def mxq(x, axis, fmt="e4m3"):
    dtype, down = {"e4m3": (ml_dtypes.float8_e4m3fn, 7), "e5m2": (ml_dtypes.float8_e5m2, 14)}[fmt]
    v = np.moveaxis(np.asarray(x, np.float32).astype(ml_dtypes.bfloat16).astype(np.float64), axis, -1)
    blocks = v.reshape(v.shape[:-1] + (-1, 32))
    amax = np.abs(blocks).max(-1, keepdims=True)
    byte = np.maximum(np.where(amax > 0, np.frexp(amax)[1] - 1 + 127, 0) - down, 1)
    scale = np.exp2(byte - 127.0)
    codes = (blocks / scale).astype(np.float32).astype(dtype).astype(np.float64)
    return np.moveaxis((codes * scale).reshape(v.shape), -1, axis)


WIDE = False


def mx_kscale(k):
    if not WIDE:
        return np.ones(k)
    levels = np.array([10, -10, 5, -5, 0])
    if k % 512:
        return np.exp2(np.random.permutation(np.resize(levels, k // 32))).repeat(32)
    a = np.empty((k // 512, 16))
    for p in range(k // 512):
        a[p, :8] = np.random.permutation(np.resize(levels, 8))
        for g in range(8):
            far = levels[np.abs(levels - a[p, g]) >= 10]
            a[p, g + 8] = far[np.random.randint(len(far))]
    return np.exp2(a.ravel()).repeat(32)


def f64(x):
    return np.asarray(x).astype(np.float64)


def striped(idx):
    return np.tile(idx.reshape(-1, 16).T, (8, 1)).astype(np.uint16)


def unstriped(offs):
    return offs[:16].T.reshape(-1).astype(np.int64)


def striped8(idx):
    return np.concatenate([x.reshape(-1, 16).T for x in idx]).astype(np.uint16)


def runs(offs, k):
    lists = np.stack([offs[16 * r : 16 * r + 16].T.reshape(-1) for r in range(8)]).astype(np.int64)
    return lists[np.arange(k) % 512 // 64]


def pack_weight(w):
    k, n = w.shape
    w = f64(np.asarray(w, np.float32).astype(ml_dtypes.bfloat16)).reshape(k // 32, 32, n)
    amax = np.abs(w).max(1)
    byte = np.clip(np.where(amax > 0, np.frexp(amax)[1] - 1 + 127 - 7, 1), 1, 254)
    scaled = (w * np.exp2(127.0 - byte)[:, None, :]).reshape(k, n).astype(np.float32)
    words = np.ascontiguousarray(scaled.reshape(k // 512, 128, 4, n).transpose(0, 1, 3, 2)).astype(ml_dtypes.float8_e4m3fn).view(np.uint8)
    return words, np.ascontiguousarray(byte.astype(np.uint8).reshape(k // 512, 16, n))


def unpack_weight(words, scales):
    g, p, n, _ = words.shape
    vals = np.ascontiguousarray(words).view(ml_dtypes.float8_e4m3fn).astype(np.float64) * np.repeat(np.exp2(scales.astype(np.float64) - 127.0), 8, axis=1)[..., None]
    return vals.transpose(0, 1, 3, 2).reshape(g * 512, n)

def planes(y):
    n, m = y.shape
    v = y.astype(np.float32).astype(ml_dtypes.bfloat16).astype(np.float64).reshape(n // 32, 32, m)
    top = np.abs(v).max(1)
    byte = np.clip(np.where(top > 0, np.frexp(top)[1] - 1 + 127 - 7, 1), 1, 254)
    codes = (v * np.exp2(127.0 - byte)[:, None, :]).reshape(n, m).astype(np.float32).astype(ml_dtypes.float8_e4m3fn).view(np.uint8)
    words = codes.reshape(n // 512, 128, 4, m).transpose(0, 1, 3, 2)
    return np.ascontiguousarray(words), np.ascontiguousarray(byte.astype(np.uint8).reshape(n // 512, 16, m))


K, T, S, V, H, W = 512, 2048, 512, 512, 512, 384


def setup_inputs():
    n = np.random.standard_normal
    s = mx_kscale(K)[:, None]
    u = mx_kscale(S)
    packed_xT = pack_weight(n((K, T)) * s)
    packed_w1 = pack_weight(n((K, H)) / np.sqrt(K) / s)
    packed_w2 = pack_weight(n((K, H)) / np.sqrt(K) / s)
    return {
        "x_words": packed_xT[0],
        "x_scales": packed_xT[1],
        "w1_words": packed_w1[0],
        "w1_scales": packed_w1[1],
        "w2_words": packed_w2[0],
        "w2_scales": packed_w2[1],
        "ga": (np.random.uniform(0.5, 1.5, (H, 1)) * u[:, None]).astype(np.float32),
        "gb": (np.random.uniform(0.5, 1.5, (H, 1)) / u[:, None]).astype(np.float32),
        "offs": striped8(np.random.randint(0, T, (8, S))),
        "two": striped(np.random.permutation(T)[:V]),
        "n1": striped8(np.stack([np.random.permutation(S) for _ in range(8)])),
        "n2": striped8(np.stack([np.random.permutation(S) for _ in range(8)])),
        "n3": striped(np.random.permutation(V)[:W]),
        "n4": striped(np.random.permutation(V)[:W]),
        "n5": striped8(np.stack([np.random.permutation(V) for _ in range(8)])),
        "n6": striped8(np.stack([np.random.permutation(V) for _ in range(8)])),
    }


def reference(x_words, x_scales, w1_words, w1_scales, w2_words, w2_scales, ga, gb, offs, two, n1, n2, n3, n4, n5, n6):
    xq = unpack_weight(x_words, x_scales)[np.arange(K)[:, None], runs(offs, K)]
    a = unpack_weight(w1_words, w1_scales).T @ xq
    st = np.maximum(a, a[np.arange(H)[:, None], runs(n1, H)])
    z = f64(ga) * (np.minimum(st, st[np.arange(H)[:, None], runs(n2, H)]))
    x_two = unpack_weight(x_words, x_scales)[:, unstriped(two)]
    b = unpack_weight(w2_words, w2_scales).T @ x_two
    old = b[:, unstriped(n3)]
    pa = b[:, unstriped(n4)]
    ra = old - (0.5 * pa)
    ds = b.copy()
    ds[:, unstriped(n3)] = ra
    z2 = f64(gb) * ds
    s = 0.0625 * ((mxq(z, 0, "e4m3").T @ mxq(z2, 0, "e4m3")))
    out_0 = s[np.arange(S)[:, None], runs(n5, S)] + 0.75 * (s[np.arange(S)[:, None], runs(n6, S)])
    return (out_0,) + planes(out_0)

@@ -1,0 +1,262 @@
+from contextlib import ExitStack
+
+import concourse.mybir as mybir
+
+K, T, S, V, H, W = 512, 2048, 512, 512, 512, 384
+FLOPS = 3 * 2 * 512 * 512 * 512
+
+F32 = mybir.dt.float32
+BF16 = mybir.dt.bfloat16
+I32 = mybir.dt.int32
+U32 = mybir.dt.uint32
+U16 = mybir.dt.uint16
+U8 = mybir.dt.uint8
+FP8X4 = mybir.dt.float8_e4m3fn_x4
+ALU = mybir.AluOpType
+ACT = mybir.ActivationFunctionType
+
+P = 128
+PACK = 4
+HALF = 256
+GROUP = 16
+SCATTER_COLS = 768
+
+
+def tile_picked_hkqhopmnkdifsum_none_po_kernel(
+    tc, x_words, x_scales, w1_words, w1_scales, w2_words, w2_scales, ga, gb,
+    offs, two, n1, n2, n3, n4, n5, n6, out_0, out_1, out_2,
+):
+    nc = tc.nc
+    with ExitStack() as ctx:
+        keep = ctx.enter_context(tc.tile_pool(name="keep", bufs=1))
+        psum = ctx.enter_context(tc.psum_pool(name="psum", bufs=1))
+
+        def sb(name, shape, dtype, tag=""):
+            return keep.tile(shape, dtype, name=name, align_bytes=64, tag=tag or name)
+
+        def load_list(name, src):
+            tile = keep.tile(list(src.shape), U16, name=name)
+            nc.sync.dma_start(tile[:], src)
+            return tile
+
+        def words_of(src):
+            return src[0].rearrange("p c r -> p (c r)").bitcast(I32)
+
+        def half_list(tile, h):
+            cols = HALF // GROUP
+            return tile[:, h * cols : (h + 1) * cols]
+
+        def half(h):
+            return slice(h * HALF, (h + 1) * HALF)
+
+        two_sb = load_list("two_sb", two)
+        xs = sb("xs", [P, T], U8)
+        xs_rows = x_scales[0].bitcast(I32)
+        for q in range(4):
+            nc.sync.dma_start(
+                out=xs[32 * q : 32 * q + 32, :].bitcast(I32),
+                in_=xs_rows[4 * q : 4 * q + 4, :].unsqueeze(0).to_broadcast([8, 4, T // 4]),
+            )
+        offs_sb = load_list("offs_sb", offs)
+        xw = sb("xw", [P, T], U32)
+        nc.sync.dma_start(out=xw[:].bitcast(I32), in_=words_of(x_words))
+        w2_raw = sb("w2_raw", [P, H], I32)
+        nc.sync.dma_start(out=w2_raw[:], in_=words_of(w2_words))
+
+        def load_weight_scales(name, src, queue):
+            tile = sb(name, [P, H], U8, tag=name)
+            nc.vector.memset(tile[:].bitcast(I32), 0)
+            rows = src[0].bitcast(I32)
+            for q in range(4):
+                queue.dma_start(out=tile[32 * q : 32 * q + 4, :].bitcast(I32), in_=rows[4 * q : 4 * q + 4, :])
+            return tile
+
+        w2s_raw = load_weight_scales("w2s_raw", w2_scales, nc.scalar)
+        g_raw = sb("g_raw", [P, 16], F32)
+        nc.sync.dma_start(out=g_raw[:, 0:4], in_=ga.rearrange("(p t) o -> p (t o)", t=PACK))
+        nc.sync.dma_start(out=g_raw[:, 8:12], in_=gb.rearrange("(p t) o -> p (t o)", t=PACK))
+        n4_sb = load_list("n4_sb", n4)
+        n3_sb = load_list("n3_sb", n3)
+        w1_raw = sb("w1_raw", [P, H], I32)
+        nc.sync.dma_start(out=w1_raw[:], in_=words_of(w1_words))
+        w1s_raw = load_weight_scales("w1s_raw", w1_scales, nc.sync)
+        n1_sb = load_list("n1_sb", n1)
+        n2_sb = load_list("n2_sb", n2)
+        n5_sb = load_list("n5_sb", n5)
+        n6_sb = load_list("n6_sb", n6)
+
+        xt_s = sb("xt_s", [P, V], U8)
+        nc.vector.tensor_copy(xt_s[:], xs[:].indirect(two_sb[:]))
+        xq_s_raw = sb("xq_s_raw", [P, S], U8)
+        nc.vector.tensor_copy(xq_s_raw[:], xs[:].indirect(offs_sb[:]))
+        xq_s = sb("xq_s", [P, S], U8)
+        nc.vector.tensor_copy(xq_s[:].bitcast(I32), xq_s_raw[:].bitcast(I32))
+        for j in (2, 3):
+            nc.sync.dma_start(
+                out=xq_s[j:P:32, :].bitcast(I32), in_=xq_s_raw[GROUP + j : P : 32, :].bitcast(I32)
+            )
+
+        def deal(dst, src):
+            nc.vector.tensor_copy(
+                out=dst.rearrange("p (t m) -> p m t", t=PACK), in_=src.rearrange("p (m t) -> p m t", t=PACK)
+            )
+
+        w2_w = sb("w2_w", [P, H], I32)
+        w2_s = sb("w2_s", [P, H], U8)
+        w1_w = sb("w1_w", [P, H], I32)
+        w1_s = sb("w1_s", [P, H], U8)
+        deal(w2_w[:], w2_raw[:])
+        deal(w2_s[:], w2s_raw[:])
+        xt_w = sb("xt_w", [P, V], U32)
+        nc.vector.tensor_copy(xt_w[:], xw[:].indirect(two_sb[:]))
+
+        ga_abs = sb("ga_abs", [P, PACK], F32)
+        nc.scalar.activation(ga_abs[:], g_raw[:, 0:4], ACT.Abs)
+        sgn = sb("sgn", [P, PACK], F32)
+        nc.vector.tensor_scalar(sgn[:], g_raw[:, 0:4], 0.0, 2.0, ALU.is_ge, ALU.mult)
+        gb_signed = sb("gb_signed", [P, PACK], F32)
+        nc.vector.scalar_tensor_tensor(gb_signed[:], sgn[:], -1.0, g_raw[:, 8:12], ALU.add, ALU.mult)
+
+        def product(name, tag, lw, ls, rw, rs, t):
+            acc = psum.tile([P, 512], F32, name=name, tag=tag)
+            cols = slice(t * P, (t + 1) * P)
+            nc.tensor.matmul_mx(
+                out=acc[:], lhsT=lw[:, cols].bitcast(FP8X4), lhsT_scale=ls[:, cols],
+                rhs=rw[:].bitcast(FP8X4), rhs_scale=rs[:], start=True, stop=True,
+            )
+            return acc
+
+        b_ps = [product("b_ps%d" % t, "bank%d" % t, w2_w, w2_s, xt_w, xt_s, t) for t in range(PACK)]
+
+        xq_w = sb("xq_w", [P, S], U32, tag="w2s_raw")
+        nc.vector.tensor_copy(xq_w[:], xw[:].indirect(offs_sb[:]))
+        deal(w1_w[:], w1_raw[:])
+        deal(w1_s[:], w1s_raw[:])
+        a_ps = [product("a_ps%d" % t, "bank%d" % (PACK + t), w1_w, w1_s, xq_w, xq_s, t) for t in range(PACK)]
+
+        b_sb = [sb("b_sb%d" % t, [P, V], F32) for t in range(PACK)]
+        ds = [sb("ds%d" % t, [P, SCATTER_COLS], F32) for t in range(PACK)]
+        old = sb("old", [P, PACK, W], F32)
+        pa = sb("pa", [P, PACK, W], F32)
+        ds_all = sb("ds_all", [P, PACK, V], F32)
+        a_sb = [sb("a_sb%d" % t, [P, S], F32) for t in range(PACK)]
+        st = [sb("st%d" % t, [P, S], F32) for t in range(PACK)]
+        g1 = sb("g1", [P, PACK, S], F32)
+        g2 = sb("g2", [P, PACK, S], F32)
+        z_rows = sb("z_rows", [P, PACK, S], BF16)
+
+        def evac_b_scalar(t):
+            nc.scalar.activation(b_sb[t][:], b_ps[t][:], ACT.Copy, scale=gb_signed[:, t : t + 1])
+
+        def evac_b_vector(t):
+            nc.vector.tensor_scalar(b_sb[t][:], b_ps[t][:], gb_signed[:, t : t + 1], None, ALU.mult)
+
+        def copy_base(t):
+            nc.gpsimd.tensor_copy(ds[t][:, 0:V], b_sb[t][:])
+
+        def fetch_b(t):
+            nc.scalar.activation(pa[:, t, :], b_sb[t][:].indirect(n4_sb[:]), ACT.Copy, scale=-0.5)
+            nc.scalar.activation(old[:, t, :], b_sb[t][:].indirect(n3_sb[:]), ACT.Copy)
+
+        def scatter(t):
+            nc.vector.tensor_tensor(ds[t][:].indirect(n3_sb[:]), old[:, t, :], pa[:, t, :], ALU.add)
+            nc.sync.dma_start(out=ds_all[:, t, :], in_=ds[t][:, 0:V])
+
+        def evac_a(t):
+            nc.scalar.activation(a_sb[t][:], a_ps[t][:], ACT.Copy, scale=ga_abs[:, t : t + 1])
+
+        def fetch_n1(t):
+            for h in range(2):
+                nc.scalar.activation(g1[:, t, half(h)], a_sb[t][:].indirect(half_list(n1_sb, h)), ACT.Copy)
+
+        def larger(t):
+            nc.vector.tensor_tensor(st[t][:], a_sb[t][:], g1[:, t, :], ALU.max)
+
+        def fetch_n2(t, h):
+            nc.scalar.activation(g2[:, t, half(h)], st[t][:].indirect(half_list(n2_sb, h)), ACT.Copy)
+
+        def smaller(t, cols):
+            nc.vector.tensor_tensor(z_rows[:, t, cols], st[t][:, cols], g2[:, t, cols], ALU.min)
+
+        whole = slice(0, S)
+        evac_b_scalar(0)
+        copy_base(0)
+        for t in range(1, PACK):
+            evac_b_vector(t)
+            copy_base(t)
+        for t in range(PACK):
+            fetch_b(t)
+            scatter(t)
+        for t in range(PACK):
+            evac_a(t)
+            fetch_n1(t)
+            larger(t)
+
+        z2_in = sb("z2_in", [P, V * PACK], BF16)
+        nc.vector.tensor_copy(
+            out=z2_in[:].rearrange("p (c i t) -> p c t i", i=4, t=PACK),
+            in_=ds_all[:].rearrange("p t (c i) -> p c t i", i=4),
+        )
+        z2_w = sb("z2_w", [P, V], U32)
+        z2_s = sb("z2_s", [P, V], U8)
+        nc.vector.quantize_mx(out=z2_w[:].bitcast(FP8X4), scales=z2_s[:], in_=z2_in[:])
+
+        z_in = sb("z_in", [P, S * PACK], BF16)
+        z_dst = z_in[:].rearrange("p (u m t) -> p u m t", u=PACK, t=PACK)
+        z_src = z_rows[:].rearrange("p t (m u) -> p u m t", u=PACK)
+        for t in (0, 1):
+            for h in range(2):
+                fetch_n2(t, h)
+            smaller(t, whole)
+        for h in range(2):
+            for t in (2, 3):
+                fetch_n2(t, h)
+                smaller(t, half(h))
+            ms = slice(h * 64, (h + 1) * 64)
+            nc.vector.tensor_copy(out=z_dst[:, :, ms, :], in_=z_src[:, :, ms, :])
+        z_w = sb("z_w", [P, S], U32)
+        z_s = sb("z_s", [P, S], U8)
+        s_ps = []
+        for u in range(PACK):
+            cols = slice(u * P, (u + 1) * P)
+            nc.vector.quantize_mx(
+                out=z_w[:, cols].bitcast(FP8X4), scales=z_s[:, cols], in_=z_in[:, u * 512 : (u + 1) * 512]
+            )
+            s_ps.append(product("s_ps%d" % u, "bank%d" % u, z_w, z_s, z2_w, z2_s, u))
+
+        s_sb = [sb("s_sb%d" % u, [P, V], F32) for u in range(PACK)]
+        g6 = sb("g6", [P, PACK, V], F32)
+        res = sb("res", [P, PACK, V], F32)
+        res_in = sb("res_in", [P, V * PACK], BF16)
+        res_w = sb("res_w", [P, V], U32)
+        res_s = sb("res_s", [P, V], U8)
+        out_rows = out_0.rearrange("(p t) v -> p t v", t=PACK)
+        out_words = words_of(out_1)
+        out_scale_rows = out_2[0].bitcast(I32)
+
+        for h in range(2):
+            for u in range(PACK):
+                if h == 0:
+                    if u == 1:
+                        nc.vector.tensor_scalar(s_sb[u][:], s_ps[u][:], 0.0625, None, ALU.mult)
+                    else:
+                        nc.scalar.activation(s_sb[u][:], s_ps[u][:], ACT.Copy, scale=0.0625)
+                nc.scalar.activation(
+                    g6[:, u, half(h)], s_sb[u][:].indirect(half_list(n6_sb, h)), ACT.Copy, scale=0.75
+                )
+                nc.vector.tensor_tensor(
+                    res[:, u, half(h)], s_sb[u][:].indirect(half_list(n5_sb, h)), g6[:, u, half(h)], ALU.add
+                )
+            nc.sync.dma_start(out=out_rows[:, :, half(h)], in_=res[:, :, half(h)])
+            piece = res_in[:, h * HALF * PACK : (h + 1) * HALF * PACK]
+            nc.vector.tensor_copy(
+                out=piece.rearrange("p (c i t) -> p c t i", i=4, t=PACK),
+                in_=res[:, :, half(h)].rearrange("p t (c i) -> p c t i", i=4),
+            )
+            nc.vector.quantize_mx(out=res_w[:, half(h)].bitcast(FP8X4), scales=res_s[:, half(h)], in_=piece)
+            nc.sync.dma_start(out=out_words[:, half(h)], in_=res_w[:, half(h)].bitcast(I32))
+        for q in range(4):
+            queue = nc.scalar if q % 2 == 0 else nc.sync
+            queue.dma_start(
+                out=out_scale_rows[4 * q : 4 * q + 4, :], in_=res_s[32 * q : 32 * q + 4, :].bitcast(I32)
+            )

@@ -49,37 +49,32 @@ def tile_picked_hkqhopmnkdifsum_none_po_kernel(
         def half(h):
             return slice(h * HALF, (h + 1) * HALF)
 
+        def load_scale_rows(name, src, width):
+            tile = sb(name, [P, width], U8)
+            rows = src[0].bitcast(I32)
+            for q in range(4):
+                nc.sync.dma_start(
+                    out=tile[32 * q : 32 * q + 32, :].bitcast(I32),
+                    in_=rows[4 * q : 4 * q + 4, :].unsqueeze(0).to_broadcast([8, 4, width // 4]),
+                )
+            return tile
+
         two_sb = load_list("two_sb", two)
-        xs = sb("xs", [P, T], U8)
-        xs_rows = x_scales[0].bitcast(I32)
-        for q in range(4):
-            nc.sync.dma_start(
-                out=xs[32 * q : 32 * q + 32, :].bitcast(I32),
-                in_=xs_rows[4 * q : 4 * q + 4, :].unsqueeze(0).to_broadcast([8, 4, T // 4]),
-            )
+        xs = load_scale_rows("xs", x_scales, T)
         offs_sb = load_list("offs_sb", offs)
         xw = sb("xw", [P, T], U32)
         nc.sync.dma_start(out=xw[:].bitcast(I32), in_=words_of(x_words))
         w2_raw = sb("w2_raw", [P, H], I32)
         nc.sync.dma_start(out=w2_raw[:], in_=words_of(w2_words))
-
-        def load_weight_scales(name, src, queue):
-            tile = sb(name, [P, H], U8, tag=name)
-            nc.vector.memset(tile[:].bitcast(I32), 0)
-            rows = src[0].bitcast(I32)
-            for q in range(4):
-                queue.dma_start(out=tile[32 * q : 32 * q + 4, :].bitcast(I32), in_=rows[4 * q : 4 * q + 4, :])
-            return tile
-
-        w2s_raw = load_weight_scales("w2s_raw", w2_scales, nc.scalar)
+        w2s_raw = load_scale_rows("w2s_raw", w2_scales, H)
         g_raw = sb("g_raw", [P, 16], F32)
-        nc.sync.dma_start(out=g_raw[:, 0:4], in_=ga.rearrange("(p t) o -> p (t o)", t=PACK))
         nc.sync.dma_start(out=g_raw[:, 8:12], in_=gb.rearrange("(p t) o -> p (t o)", t=PACK))
-        n4_sb = load_list("n4_sb", n4)
-        n3_sb = load_list("n3_sb", n3)
+        nc.sync.dma_start(out=g_raw[:, 0:4], in_=ga.rearrange("(p t) o -> p (t o)", t=PACK))
         w1_raw = sb("w1_raw", [P, H], I32)
         nc.sync.dma_start(out=w1_raw[:], in_=words_of(w1_words))
-        w1s_raw = load_weight_scales("w1s_raw", w1_scales, nc.sync)
+        w1s_raw = load_scale_rows("w1s_raw", w1_scales, H)
+        n4_sb = load_list("n4_sb", n4)
+        n3_sb = load_list("n3_sb", n3)
         n1_sb = load_list("n1_sb", n1)
         n2_sb = load_list("n2_sb", n2)
         n5_sb = load_list("n5_sb", n5)
@@ -92,7 +87,7 @@ def tile_picked_hkqhopmnkdifsum_none_po_kernel(
         xq_s = sb("xq_s", [P, S], U8)
         nc.vector.tensor_copy(xq_s[:].bitcast(I32), xq_s_raw[:].bitcast(I32))
         for j in (2, 3):
-            nc.sync.dma_start(
+            nc.gpsimd.dma_start(
                 out=xq_s[j:P:32, :].bitcast(I32), in_=xq_s_raw[GROUP + j : P : 32, :].bitcast(I32)
             )
 
@@ -105,10 +100,10 @@ def tile_picked_hkqhopmnkdifsum_none_po_kernel(
         w2_s = sb("w2_s", [P, H], U8)
         w1_w = sb("w1_w", [P, H], I32)
         w1_s = sb("w1_s", [P, H], U8)
-        deal(w2_w[:], w2_raw[:])
-        deal(w2_s[:], w2s_raw[:])
         xt_w = sb("xt_w", [P, V], U32)
         nc.vector.tensor_copy(xt_w[:], xw[:].indirect(two_sb[:]))
+        deal(w2_w[:], w2_raw[:])
+        deal(w2_s[:], w2s_raw[:])
 
         ga_abs = sb("ga_abs", [P, PACK], F32)
         nc.scalar.activation(ga_abs[:], g_raw[:, 0:4], ACT.Abs)
@@ -152,7 +147,7 @@ def tile_picked_hkqhopmnkdifsum_none_po_kernel(
             nc.vector.tensor_scalar(b_sb[t][:], b_ps[t][:], gb_signed[:, t : t + 1], None, ALU.mult)
 
         def copy_base(t):
-            nc.gpsimd.tensor_copy(ds[t][:, 0:V], b_sb[t][:])
+            nc.vector.tensor_copy(ds[t][:, 0:V], b_sb[t][:])
 
         def fetch_b(t):
             nc.scalar.activation(pa[:, t, :], b_sb[t][:].indirect(n4_sb[:]), ACT.Copy, scale=-0.5)
@@ -179,12 +174,12 @@ def tile_picked_hkqhopmnkdifsum_none_po_kernel(
             nc.vector.tensor_tensor(z_rows[:, t, cols], st[t][:, cols], g2[:, t, cols], ALU.min)
 
         whole = slice(0, S)
-        evac_b_scalar(0)
-        copy_base(0)
-        for t in range(1, PACK):
-            evac_b_vector(t)
-            copy_base(t)
         for t in range(PACK):
+            if t == 0:
+                evac_b_scalar(t)
+            else:
+                evac_b_vector(t)
+            copy_base(t)
             fetch_b(t)
             scatter(t)
         for t in range(PACK):
@@ -192,28 +187,27 @@ def tile_picked_hkqhopmnkdifsum_none_po_kernel(
             fetch_n1(t)
             larger(t)
 
-        z2_in = sb("z2_in", [P, V * PACK], BF16)
+        z2_in = g1[:, 2:4, :].rearrange("p a c -> p (a c)").bitcast(BF16)
         nc.vector.tensor_copy(
-            out=z2_in[:].rearrange("p (c i t) -> p c t i", i=4, t=PACK),
+            out=z2_in.rearrange("p (c i t) -> p c t i", i=4, t=PACK),
             in_=ds_all[:].rearrange("p t (c i) -> p c t i", i=4),
         )
-        z2_w = sb("z2_w", [P, V], U32)
-        z2_s = sb("z2_s", [P, V], U8)
-        nc.vector.quantize_mx(out=z2_w[:].bitcast(FP8X4), scales=z2_s[:], in_=z2_in[:])
 
         z_in = sb("z_in", [P, S * PACK], BF16)
         z_dst = z_in[:].rearrange("p (u m t) -> p u m t", u=PACK, t=PACK)
         z_src = z_rows[:].rearrange("p t (m u) -> p u m t", u=PACK)
-        for t in (0, 1):
+        for t in range(PACK - 1):
             for h in range(2):
                 fetch_n2(t, h)
             smaller(t, whole)
         for h in range(2):
-            for t in (2, 3):
-                fetch_n2(t, h)
-                smaller(t, half(h))
-            ms = slice(h * 64, (h + 1) * 64)
-            nc.vector.tensor_copy(out=z_dst[:, :, ms, :], in_=z_src[:, :, ms, :])
+            fetch_n2(PACK - 1, h)
+            smaller(PACK - 1, half(h))
+        nc.scalar.copy(out=z_dst[:, :, 0:64, :], in_=z_src[:, :, 0:64, :])
+        z2_w = sb("z2_w", [P, V], U32)
+        z2_s = sb("z2_s", [P, V], U8)
+        nc.vector.quantize_mx(out=z2_w[:].bitcast(FP8X4), scales=z2_s[:], in_=z2_in)
+        nc.vector.tensor_copy(out=z_dst[:, :, 64:128, :], in_=z_src[:, :, 64:128, :])
         z_w = sb("z_w", [P, S], U32)
         z_s = sb("z_s", [P, S], U8)
         s_ps = []
@@ -234,25 +228,28 @@ def tile_picked_hkqhopmnkdifsum_none_po_kernel(
         out_words = words_of(out_1)
         out_scale_rows = out_2[0].bitcast(I32)
 
-        for h in range(2):
-            for u in range(PACK):
-                if h == 0:
-                    if u == 1:
-                        nc.vector.tensor_scalar(s_sb[u][:], s_ps[u][:], 0.0625, None, ALU.mult)
-                    else:
-                        nc.scalar.activation(s_sb[u][:], s_ps[u][:], ACT.Copy, scale=0.0625)
+        for u in range(PACK):
+            if u in (1, 2):
+                nc.vector.tensor_scalar(s_sb[u][:], s_ps[u][:], 0.0625, None, ALU.mult)
+            else:
+                nc.scalar.activation(s_sb[u][:], s_ps[u][:], ACT.Copy, scale=0.0625)
+            for h in range(2):
                 nc.scalar.activation(
                     g6[:, u, half(h)], s_sb[u][:].indirect(half_list(n6_sb, h)), ACT.Copy, scale=0.75
                 )
                 nc.vector.tensor_tensor(
                     res[:, u, half(h)], s_sb[u][:].indirect(half_list(n5_sb, h)), g6[:, u, half(h)], ALU.add
                 )
-            nc.sync.dma_start(out=out_rows[:, :, half(h)], in_=res[:, :, half(h)])
+            nc.sync.dma_start(out=out_rows[:, u, :], in_=res[:, u, :])
+        for h in range(2):
             piece = res_in[:, h * HALF * PACK : (h + 1) * HALF * PACK]
-            nc.vector.tensor_copy(
+            weave = nc.scalar.copy if h == 0 else nc.vector.tensor_copy
+            weave(
                 out=piece.rearrange("p (c i t) -> p c t i", i=4, t=PACK),
                 in_=res[:, :, half(h)].rearrange("p t (c i) -> p c t i", i=4),
             )
+        for h in range(2):
+            piece = res_in[:, h * HALF * PACK : (h + 1) * HALF * PACK]
             nc.vector.quantize_mx(out=res_w[:, half(h)].bitcast(FP8X4), scales=res_s[:, half(h)], in_=piece)
             nc.sync.dma_start(out=out_words[:, half(h)], in_=res_w[:, half(h)].bitcast(I32))
         for q in range(4):

from contextlib import ExitStack

import concourse.mybir as mybir

K, T, S, V, H, W = 512, 2048, 512, 512, 512, 384
FLOPS = 3 * 2 * 512 * 512 * 512

F32 = mybir.dt.float32
BF16 = mybir.dt.bfloat16
I32 = mybir.dt.int32
U32 = mybir.dt.uint32
U16 = mybir.dt.uint16
U8 = mybir.dt.uint8
FP8X4 = mybir.dt.float8_e4m3fn_x4
ALU = mybir.AluOpType
ACT = mybir.ActivationFunctionType

P = 128
PACK = 4
HALF = 256
GROUP = 16
SCATTER_COLS = 768


def tile_picked_hkqhopmnkdifsum_none_po_kernel(
    tc, x_words, x_scales, w1_words, w1_scales, w2_words, w2_scales, ga, gb,
    offs, two, n1, n2, n3, n4, n5, n6, out_0, out_1, out_2,
):
    nc = tc.nc
    with ExitStack() as ctx:
        keep = ctx.enter_context(tc.tile_pool(name="keep", bufs=1))
        psum = ctx.enter_context(tc.psum_pool(name="psum", bufs=1))

        def sb(name, shape, dtype, tag=""):
            return keep.tile(shape, dtype, name=name, align_bytes=64, tag=tag or name)

        def load_list(name, src):
            tile = keep.tile(list(src.shape), U16, name=name)
            nc.sync.dma_start(tile[:], src)
            return tile

        def words_of(src):
            return src[0].rearrange("p c r -> p (c r)").bitcast(I32)

        def half_list(tile, h):
            cols = HALF // GROUP
            return tile[:, h * cols : (h + 1) * cols]

        def half(h):
            return slice(h * HALF, (h + 1) * HALF)

        def load_scale_rows(name, src, width):
            tile = sb(name, [P, width], U8)
            rows = src[0].bitcast(I32)
            for q in range(4):
                nc.sync.dma_start(
                    out=tile[32 * q : 32 * q + 32, :].bitcast(I32),
                    in_=rows[4 * q : 4 * q + 4, :].unsqueeze(0).to_broadcast([8, 4, width // 4]),
                )
            return tile

        two_sb = load_list("two_sb", two)
        xs = load_scale_rows("xs", x_scales, T)
        offs_sb = load_list("offs_sb", offs)
        xw = sb("xw", [P, T], U32)
        nc.sync.dma_start(out=xw[:].bitcast(I32), in_=words_of(x_words))
        w2_raw = sb("w2_raw", [P, H], I32)
        nc.sync.dma_start(out=w2_raw[:], in_=words_of(w2_words))
        w2s_raw = load_scale_rows("w2s_raw", w2_scales, H)
        g_raw = sb("g_raw", [P, 16], F32)
        nc.sync.dma_start(out=g_raw[:, 8:12], in_=gb.rearrange("(p t) o -> p (t o)", t=PACK))
        nc.sync.dma_start(out=g_raw[:, 0:4], in_=ga.rearrange("(p t) o -> p (t o)", t=PACK))
        w1_raw = sb("w1_raw", [P, H], I32)
        nc.sync.dma_start(out=w1_raw[:], in_=words_of(w1_words))
        w1s_raw = load_scale_rows("w1s_raw", w1_scales, H)
        n4_sb = load_list("n4_sb", n4)
        n3_sb = load_list("n3_sb", n3)
        n1_sb = load_list("n1_sb", n1)
        n2_sb = load_list("n2_sb", n2)
        n5_sb = load_list("n5_sb", n5)
        n6_sb = load_list("n6_sb", n6)

        xt_s = sb("xt_s", [P, V], U8)
        nc.vector.tensor_copy(xt_s[:], xs[:].indirect(two_sb[:]))
        xq_s_raw = sb("xq_s_raw", [P, S], U8)
        nc.vector.tensor_copy(xq_s_raw[:], xs[:].indirect(offs_sb[:]))
        xq_s = sb("xq_s", [P, S], U8)
        nc.vector.tensor_copy(xq_s[:].bitcast(I32), xq_s_raw[:].bitcast(I32))
        for j in (2, 3):
            nc.gpsimd.dma_start(
                out=xq_s[j:P:32, :].bitcast(I32), in_=xq_s_raw[GROUP + j : P : 32, :].bitcast(I32)
            )

        def deal(dst, src):
            nc.vector.tensor_copy(
                out=dst.rearrange("p (t m) -> p m t", t=PACK), in_=src.rearrange("p (m t) -> p m t", t=PACK)
            )

        w2_w = sb("w2_w", [P, H], I32)
        w2_s = sb("w2_s", [P, H], U8)
        w1_w = sb("w1_w", [P, H], I32)
        w1_s = sb("w1_s", [P, H], U8)
        xt_w = sb("xt_w", [P, V], U32)
        nc.vector.tensor_copy(xt_w[:], xw[:].indirect(two_sb[:]))
        deal(w2_w[:], w2_raw[:])
        deal(w2_s[:], w2s_raw[:])

        ga_abs = sb("ga_abs", [P, PACK], F32)
        nc.scalar.activation(ga_abs[:], g_raw[:, 0:4], ACT.Abs)
        sgn = sb("sgn", [P, PACK], F32)
        nc.vector.tensor_scalar(sgn[:], g_raw[:, 0:4], 0.0, 2.0, ALU.is_ge, ALU.mult)
        gb_signed = sb("gb_signed", [P, PACK], F32)
        nc.vector.scalar_tensor_tensor(gb_signed[:], sgn[:], -1.0, g_raw[:, 8:12], ALU.add, ALU.mult)

        def product(name, tag, lw, ls, rw, rs, t):
            acc = psum.tile([P, 512], F32, name=name, tag=tag)
            cols = slice(t * P, (t + 1) * P)
            nc.tensor.matmul_mx(
                out=acc[:], lhsT=lw[:, cols].bitcast(FP8X4), lhsT_scale=ls[:, cols],
                rhs=rw[:].bitcast(FP8X4), rhs_scale=rs[:], start=True, stop=True,
            )
            return acc

        b_ps = [product("b_ps%d" % t, "bank%d" % t, w2_w, w2_s, xt_w, xt_s, t) for t in range(PACK)]

        xq_w = sb("xq_w", [P, S], U32, tag="w2s_raw")
        nc.vector.tensor_copy(xq_w[:], xw[:].indirect(offs_sb[:]))
        deal(w1_w[:], w1_raw[:])
        deal(w1_s[:], w1s_raw[:])
        a_ps = [product("a_ps%d" % t, "bank%d" % (PACK + t), w1_w, w1_s, xq_w, xq_s, t) for t in range(PACK)]

        b_sb = [sb("b_sb%d" % t, [P, V], F32) for t in range(PACK)]
        ds = [sb("ds%d" % t, [P, SCATTER_COLS], F32) for t in range(PACK)]
        old = sb("old", [P, PACK, W], F32)
        pa = sb("pa", [P, PACK, W], F32)
        ds_all = sb("ds_all", [P, PACK, V], F32)
        a_sb = [sb("a_sb%d" % t, [P, S], F32) for t in range(PACK)]
        st = [sb("st%d" % t, [P, S], F32) for t in range(PACK)]
        g1 = sb("g1", [P, PACK, S], F32)
        g2 = sb("g2", [P, PACK, S], F32)
        z_rows = sb("z_rows", [P, PACK, S], BF16)

        def evac_b_scalar(t):
            nc.scalar.activation(b_sb[t][:], b_ps[t][:], ACT.Copy, scale=gb_signed[:, t : t + 1])

        def evac_b_vector(t):
            nc.vector.tensor_scalar(b_sb[t][:], b_ps[t][:], gb_signed[:, t : t + 1], None, ALU.mult)

        def copy_base(t):
            nc.vector.tensor_copy(ds[t][:, 0:V], b_sb[t][:])

        def fetch_b(t):
            nc.scalar.activation(pa[:, t, :], b_sb[t][:].indirect(n4_sb[:]), ACT.Copy, scale=-0.5)
            nc.scalar.activation(old[:, t, :], b_sb[t][:].indirect(n3_sb[:]), ACT.Copy)

        def scatter(t):
            nc.vector.tensor_tensor(ds[t][:].indirect(n3_sb[:]), old[:, t, :], pa[:, t, :], ALU.add)
            nc.sync.dma_start(out=ds_all[:, t, :], in_=ds[t][:, 0:V])

        def evac_a(t):
            nc.scalar.activation(a_sb[t][:], a_ps[t][:], ACT.Copy, scale=ga_abs[:, t : t + 1])

        def fetch_n1(t):
            for h in range(2):
                nc.scalar.activation(g1[:, t, half(h)], a_sb[t][:].indirect(half_list(n1_sb, h)), ACT.Copy)

        def larger(t):
            nc.vector.tensor_tensor(st[t][:], a_sb[t][:], g1[:, t, :], ALU.max)

        def fetch_n2(t, h):
            nc.scalar.activation(g2[:, t, half(h)], st[t][:].indirect(half_list(n2_sb, h)), ACT.Copy)

        def smaller(t, cols):
            nc.vector.tensor_tensor(z_rows[:, t, cols], st[t][:, cols], g2[:, t, cols], ALU.min)

        whole = slice(0, S)
        for t in range(PACK):
            if t == 0:
                evac_b_scalar(t)
            else:
                evac_b_vector(t)
            copy_base(t)
            fetch_b(t)
            scatter(t)
        for t in range(PACK):
            evac_a(t)
            fetch_n1(t)
            larger(t)

        z2_in = g1[:, 2:4, :].rearrange("p a c -> p (a c)").bitcast(BF16)
        nc.vector.tensor_copy(
            out=z2_in.rearrange("p (c i t) -> p c t i", i=4, t=PACK),
            in_=ds_all[:].rearrange("p t (c i) -> p c t i", i=4),
        )

        z_in = sb("z_in", [P, S * PACK], BF16)
        z_dst = z_in[:].rearrange("p (u m t) -> p u m t", u=PACK, t=PACK)
        z_src = z_rows[:].rearrange("p t (m u) -> p u m t", u=PACK)
        for t in range(PACK - 1):
            for h in range(2):
                fetch_n2(t, h)
            smaller(t, whole)
        for h in range(2):
            fetch_n2(PACK - 1, h)
            smaller(PACK - 1, half(h))
        nc.scalar.copy(out=z_dst[:, :, 0:64, :], in_=z_src[:, :, 0:64, :])
        z2_w = sb("z2_w", [P, V], U32)
        z2_s = sb("z2_s", [P, V], U8)
        nc.vector.quantize_mx(out=z2_w[:].bitcast(FP8X4), scales=z2_s[:], in_=z2_in)
        nc.vector.tensor_copy(out=z_dst[:, :, 64:128, :], in_=z_src[:, :, 64:128, :])
        z_w = sb("z_w", [P, S], U32)
        z_s = sb("z_s", [P, S], U8)
        s_ps = []
        for u in range(PACK):
            cols = slice(u * P, (u + 1) * P)
            nc.vector.quantize_mx(
                out=z_w[:, cols].bitcast(FP8X4), scales=z_s[:, cols], in_=z_in[:, u * 512 : (u + 1) * 512]
            )
            s_ps.append(product("s_ps%d" % u, "bank%d" % u, z_w, z_s, z2_w, z2_s, u))

        s_sb = [sb("s_sb%d" % u, [P, V], F32) for u in range(PACK)]
        g6 = sb("g6", [P, PACK, V], F32)
        res = sb("res", [P, PACK, V], F32)
        res_in = sb("res_in", [P, V * PACK], BF16)
        res_w = sb("res_w", [P, V], U32)
        res_s = sb("res_s", [P, V], U8)
        out_rows = out_0.rearrange("(p t) v -> p t v", t=PACK)
        out_words = words_of(out_1)
        out_scale_rows = out_2[0].bitcast(I32)

        for u in range(PACK):
            if u in (1, 2):
                nc.vector.tensor_scalar(s_sb[u][:], s_ps[u][:], 0.0625, None, ALU.mult)
            else:
                nc.scalar.activation(s_sb[u][:], s_ps[u][:], ACT.Copy, scale=0.0625)
            for h in range(2):
                nc.scalar.activation(
                    g6[:, u, half(h)], s_sb[u][:].indirect(half_list(n6_sb, h)), ACT.Copy, scale=0.75
                )
                nc.vector.tensor_tensor(
                    res[:, u, half(h)], s_sb[u][:].indirect(half_list(n5_sb, h)), g6[:, u, half(h)], ALU.add
                )
            nc.sync.dma_start(out=out_rows[:, u, :], in_=res[:, u, :])
        for h in range(2):
            piece = res_in[:, h * HALF * PACK : (h + 1) * HALF * PACK]
            weave = nc.scalar.copy if h == 0 else nc.vector.tensor_copy
            weave(
                out=piece.rearrange("p (c i t) -> p c t i", i=4, t=PACK),
                in_=res[:, :, half(h)].rearrange("p t (c i) -> p c t i", i=4),
            )
        for h in range(2):
            piece = res_in[:, h * HALF * PACK : (h + 1) * HALF * PACK]
            nc.vector.quantize_mx(out=res_w[:, half(h)].bitcast(FP8X4), scales=res_s[:, half(h)], in_=piece)
            nc.sync.dma_start(out=out_words[:, half(h)], in_=res_w[:, half(h)].bitcast(I32))
        for q in range(4):
            queue = nc.scalar if q % 2 == 0 else nc.sync
            queue.dma_start(
                out=out_scale_rows[4 * q : 4 * q + 4, :], in_=res_s[32 * q : 32 * q + 4, :].bitcast(I32)
            )
